import numpy as np
import ml_dtypes


def mxq(x, axis, fmt="e4m3"):
    dtype, down = {"e4m3": (ml_dtypes.float8_e4m3fn, 7), "e5m2": (ml_dtypes.float8_e5m2, 14)}[fmt]
    v = np.moveaxis(np.asarray(x, np.float32).astype(ml_dtypes.bfloat16).astype(np.float64), axis, -1)
    blocks = v.reshape(v.shape[:-1] + (-1, 32))
    amax = np.abs(blocks).max(-1, keepdims=True)
    byte = np.maximum(np.where(amax > 0, np.frexp(amax)[1] - 1 + 127, 0) - down, 1)
    scale = np.exp2(byte - 127.0)
    codes = (blocks / scale).astype(np.float32).astype(dtype).astype(np.float64)
    return np.moveaxis((codes * scale).reshape(v.shape), -1, axis)


WIDE = False


def mx_kscale(k):
    if not WIDE:
        return np.ones(k)
    levels = np.array([10, -10, 5, -5, 0])
    if k % 512:
        return np.exp2(np.random.permutation(np.resize(levels, k // 32))).repeat(32)
    a = np.empty((k // 512, 16))
    for p in range(k // 512):
        a[p, :8] = np.random.permutation(np.resize(levels, 8))
        for g in range(8):
            far = levels[np.abs(levels - a[p, g]) >= 10]
            a[p, g + 8] = far[np.random.randint(len(far))]
    return np.exp2(a.ravel()).repeat(32)


def f64(x):
    return np.asarray(x).astype(np.float64)


def striped(idx):
    return np.tile(np.asarray(idx).reshape(-1, 16).T, (8, 1)).astype(np.uint16)


def unstriped(offs):
    return offs[:16].T.reshape(-1).astype(np.int64)


def striped8(idx):
    return np.asarray(idx).reshape(8, -1, 16).transpose(0, 2, 1).reshape(128, -1).astype(np.uint16)


def unstriped8(offs):
    return offs.reshape(8, 16, -1).transpose(0, 2, 1).reshape(8, -1).astype(np.int64)


def pick8(x, idx, run):
    r = np.arange(len(x))
    return x[r[:, None], idx[r % (8 * run) // run]]


E2M1 = np.array([0.0, 0.5, 1.0, 1.5, 2.0, 3.0, 4.0, 6.0, -0.0, -0.5, -1.0, -1.5, -2.0, -3.0, -4.0, -6.0])


def pack_weight(w, fmt):
    k, n = w.shape
    w = f64(np.asarray(w, np.float32).astype(ml_dtypes.bfloat16)).reshape(k // 32, 32, n)
    amax = np.abs(w).max(1)
    if fmt == "e4m3":
        byte = np.frexp(amax)[1] - 1 + 127 - 7
    else:
        mant, ex = np.frexp(amax / 6.0)
        byte = np.where(mant > 0.5, ex, ex - 1) + 127
    byte = np.clip(np.where(amax > 0, byte, 1), 1, 254)
    scaled = (w * np.exp2(127.0 - byte)[:, None, :]).reshape(k, n).astype(np.float32)
    by_word = np.ascontiguousarray(scaled.reshape(k // 512, 128, 4, n).transpose(0, 1, 3, 2))
    if fmt == "e4m3":
        words = by_word.astype(ml_dtypes.float8_e4m3fn).view(np.uint8)
    else:
        c = by_word.astype(ml_dtypes.float4_e2m1fn).view(np.uint8) & 0xF
        words = (c[..., 0::2] | (c[..., 1::2] << 4)).reshape(k // 512, 128, 2 * n)
    return np.ascontiguousarray(words), np.ascontiguousarray(byte.astype(np.uint8).reshape(k // 512, 16, n))


def unpack_weight(words, scales, fmt):
    g, _, n = scales.shape
    words = np.ascontiguousarray(words).reshape(g, 128, n, -1)
    if fmt == "e4m3":
        vals = words.view(ml_dtypes.float8_e4m3fn).astype(np.float64)
    else:
        nib = np.empty((g, 128, n, 4), np.uint8)
        nib[..., 0::2] = words & 0xF
        nib[..., 1::2] = words >> 4
        vals = E2M1[nib]
    vals = vals * np.repeat(np.exp2(scales.astype(np.float64) - 127.0), 8, axis=1)[..., None]
    return vals.transpose(0, 1, 3, 2).reshape(g * 512, n)


K, J, R, T, C, O, D, N, S = 512, 256, 512, 512, 512, 128, 640, 256, 1024


def setup_inputs():
    n = np.random.standard_normal
    idx = np.random.permutation(T)[:J]
    idx2 = np.stack([np.random.permutation(C)[:J] for _ in range(8)])
    idx3 = np.stack([np.random.permutation(J)[:O] for _ in range(8)])
    idx4 = np.random.permutation(S)[:N]
    fk = mx_kscale(K)
    fr = mx_kscale(R)
    xtp = pack_weight(n((K, T)) * fk[:, None], "e4m3")
    wp = pack_weight(n((K, R)) * 1 / np.sqrt(K) / fk[:, None] * fr, "e2m1")
    w2p = pack_weight(n((K, R)) * 1 / np.sqrt(K) / fk[:, None] * fr, "e4m3")
    vsp = pack_weight(n((R, S)) * 1 / np.sqrt(R) / fr[:, None], "e4m3")
    return {
        "xt_words": xtp[0],
        "xt_scales": xtp[1],
        "w_words": wp[0],
        "w_scales": wp[1],
        "w2_words": w2p[0],
        "w2_scales": w2p[1],
        "sa": (np.random.uniform(0.5, 1.6, (R, 1))).astype(np.float32),
        "vs_words": vsp[0],
        "vs_scales": vsp[1],
        "offs": striped(idx),
        "offs2": striped8(idx2),
        "offs3": striped8(idx3),
        "offs4": striped(idx4),
    }


def reference(xt_words, xt_scales, w_words, w_scales, w2_words, w2_scales, sa, vs_words, vs_scales, offs, offs2, offs3, offs4):
    idx = unstriped(offs)
    idx2 = unstriped8(offs2)
    idx3 = unstriped8(offs3)
    idx4 = unstriped(offs4)
    xtu = unpack_weight(xt_words, xt_scales, "e4m3")
    wu = unpack_weight(w_words, w_scales, "e2m1")
    w2u = unpack_weight(w2_words, w2_scales, "e4m3")
    vsu = unpack_weight(vs_words, vs_scales, "e4m3")
    xtidxg = xtu[:, idx]
    a = wu.T @ xtidxg
    b = w2u.T @ xtidxg
    pw = np.zeros((R, C))
    pw[np.arange(R)[:, None], idx2[np.arange(R) % 512 // 64]] = a
    h1 = pick8(b, idx3, 64) * f64(sa)
    hid = np.concatenate([pw, h1], axis=1)
    vsidx4g = vsu[:, idx4]
    hidq = mxq(hid, 0, "e4m3")
    y = vsidx4g.T @ hidq
    return y

@@ -1,0 +1,208 @@
+from contextlib import ExitStack
+
+import concourse.mybir as mybir
+
+K, J, R, T, C, O, D, N, S = 512, 256, 512, 512, 512, 128, 640, 256, 1024
+FLOPS = 2 * (2 * K * R * J + R * N * D)
+
+F32 = mybir.dt.float32
+BF16 = mybir.dt.bfloat16
+I32 = mybir.dt.int32
+U32 = mybir.dt.uint32
+U16 = mybir.dt.uint16
+U8 = mybir.dt.uint8
+FP8X4 = mybir.dt.float8_e4m3fn_x4
+FP4X4 = mybir.dt.float4_e2m1fn_x4
+COPY = mybir.ActivationFunctionType.Copy
+MULT = mybir.AluOpType.mult
+ADD = mybir.AluOpType.add
+
+P = 128
+PACK = 4
+HALF = J // 2
+PAGE_PART = C // 2
+
+
+def tile_picked_tokens_plain_twin_pageandpicks_store_plain_kernel(
+    tc, xt_words, xt_scales, w_words, w_scales, w2_words, w2_scales, sa, vs_words, vs_scales, offs, offs2, offs3, offs4, out
+):
+    nc = tc.nc
+
+    with ExitStack() as ctx:
+        sb = ctx.enter_context(tc.tile_pool(name="sb", bufs=1))
+        ps = ctx.enter_context(tc.psum_pool(name="ps", bufs=1))
+
+        def tile(shape, dtype, name, tag=None):
+            return sb.tile(shape, dtype, name=name, tag=tag or name, align_bytes=64)
+
+        def words_of(dram):
+            return dram[0].rearrange("p n t -> p (n t)").bitcast(I32)
+
+        def load_scale_pairs(queue, stage, dram):
+            rows = dram[0].bitcast(I32).rearrange("(h g i) c -> g i h c", h=2, g=2)
+            for g in range(2):
+                queue.dma_start(out=stage[32 * g : 32 * g + 4].rearrange("i (h c) -> i h c", h=2), in_=rows[g])
+
+        def load_scale_rows(queue, plane, dram):
+            rows = dram[0].bitcast(I32)
+            for q in range(4):
+                queue.dma_start(out=plane[32 * q : 32 * q + 4, :].bitcast(I32), in_=rows[4 * q : 4 * q + 4, :])
+
+        list_x = tile([P, J // 16], U16, "list_x")
+        list_page = tile([P, J // 16], U16, "list_page")
+        list_pick = tile([P, O // 16], U16, "list_pick")
+        list_v = tile([P, N // 16], U16, "list_v")
+
+        xs_stage = tile([64, 2 * T // 4], I32, "xs_stage")
+        ws_stage = tile([P, 2 * R], U8, "ws_stage")
+        xs_all = tile([P, T], U8, "xs_all")
+        x_all = tile([P, T], U32, "x_all")
+        w_raw = tile([P, 2 * R], U8, "w_raw")
+        w2_raw = tile([P, R], U32, "w2_raw")
+        w2s_raw = tile([P, R], U8, "w2s_raw")
+        v_all = tile([P, S], U32, "v_all")
+        vs_all = tile([P, S], U8, "vs_all")
+        sa_t = tile([P, PACK], F32, "sa_t")
+        pages = [tile([P, C], F32, "page%d" % t) for t in range(PACK)]
+
+        ws_words = ws_stage[:].bitcast(I32)
+        nc.vector.memset(xs_stage[:], 0)
+        nc.gpsimd.memset(ws_words[0:64], 0)
+
+        nc.sync.dma_start(list_x[:], offs)
+        load_scale_pairs(nc.sync, xs_stage[:], xt_scales)
+        load_scale_pairs(nc.sync, ws_words, w_scales)
+        nc.sync.dma_start(out=x_all[:].bitcast(I32), in_=words_of(xt_words))
+        nc.sync.dma_start(out=w_raw[:].bitcast(I32), in_=w_words[0].bitcast(I32))
+        nc.sync.dma_start(out=w2_raw[:].bitcast(I32), in_=words_of(w2_words))
+        nc.sync.dma_start(list_page[:], offs2)
+
+        nc.vector.memset(w2s_raw[:].bitcast(I32), 0)
+        nc.vector.memset(vs_all[:].bitcast(I32), 0)
+        for page in pages:
+            nc.vector.memset(page[:], 0.0)
+
+        load_scale_rows(nc.sync, w2s_raw, w2_scales)
+        nc.sync.dma_start(list_v[:], offs4)
+        nc.sync.dma_start(out=v_all[:].bitcast(I32), in_=words_of(vs_words))
+        load_scale_rows(nc.gpsimd, vs_all, vs_scales)
+        nc.sync.dma_start(list_pick[:], offs3)
+        nc.gpsimd.dma_start(out=sa_t[:], in_=sa.rearrange("(p t) o -> p (t o)", t=PACK))
+
+        for h in range(2):
+            nc.vector.tensor_copy(xs_all[64 * h : 64 * h + 64, :].bitcast(I32), xs_stage[:, h * T // 4 : (h + 1) * T // 4])
+        nc.vector.tensor_copy(ws_words[64:128, 0 : R // 4], ws_words[0:64, R // 4 : 2 * R // 4])
+
+        x_words = tile([P, J], U32, "x_words")
+        x_scales = tile([P, J], U8, "x_scales")
+        w_first = tile([P, 2 * P], U8, "w_first")
+        ws_first = tile([P, P], U8, "ws_first")
+        w_rest = tile([P, 2 * (R - P)], U8, "w_rest")
+        ws_rest = tile([P, R - P], U8, "ws_rest")
+        w2_dealt = tile([P, R], U32, "w2_dealt")
+
+        w_by_t = w_raw[:].bitcast(U16).rearrange("p (m t) -> p t m", t=PACK)
+        ws_by_t = ws_stage[:, 0:R].rearrange("p (m t) -> p t m", t=PACK)
+
+        def gather_x(cols):
+            entries = list_x[:, cols.start // 16 : cols.stop // 16]
+            nc.vector.tensor_copy(x_scales[:, cols], xs_all[:].indirect(entries))
+            nc.vector.tensor_copy(x_words[:, cols], x_all[:].indirect(entries))
+
+        def product(acc, lhs_words, lhs_scales, rhs_words, rhs_scales):
+            nc.tensor.matmul_mx(out=acc, lhsT=lhs_words, lhsT_scale=lhs_scales, rhs=rhs_words.bitcast(FP8X4), rhs_scale=rhs_scales, start=True, stop=True)
+
+        first, second = slice(0, HALF), slice(HALF, J)
+
+        nc.scalar.copy(w_first[:].bitcast(U16), w_by_t[:, 0, :])
+        nc.vector.tensor_copy(ws_first[:], ws_by_t[:, 0, :])
+        gather_x(first)
+        bank_a0 = ps.tile([P, 512], F32, name="bank_a0")
+        product(bank_a0[:, 0:HALF], w_first[:].bitcast(FP4X4), ws_first[:], x_words[:, first], x_scales[:, first])
+        a_head = tile([P, HALF], F32, "a_head", "w2_raw")
+        nc.scalar.copy(w_rest[:].bitcast(U16).rearrange("p (t m) -> p t m", m=P), w_by_t[:, 1:PACK, :])
+        nc.scalar.copy(w2_dealt[:].rearrange("p (t m) -> p t m", t=PACK), w2_raw[:].rearrange("p (m t) -> p t m", t=PACK))
+        nc.scalar.copy(a_head[:], bank_a0[:, 0:HALF])
+        nc.scalar.activation(pages[0][:].indirect(list_page[:, 0 : HALF // 16]), a_head[:], COPY)
+
+        gather_x(second)
+        nc.vector.tensor_copy(ws_rest[:].rearrange("p (t m) -> p t m", m=P), ws_by_t[:, 1:PACK, :])
+
+        def product_a(acc, t):
+            cols = slice((t - 1) * P, t * P)
+            product(acc, w_rest[:, 2 * cols.start : 2 * cols.stop].bitcast(FP4X4), ws_rest[:, cols], x_words[:], x_scales[:])
+
+        bank_a1 = ps.tile([P, 512], F32, name="bank_a1")
+        product(bank_a1[:, 0:HALF], w_first[:].bitcast(FP4X4), ws_first[:], x_words[:, second], x_scales[:, second])
+        a_tail = tile([P, HALF], F32, "a_tail")
+        nc.vector.tensor_copy(a_tail[:], bank_a1[:, 0:HALF])
+        nc.scalar.activation(pages[0][:].indirect(list_page[:, HALF // 16 : J // 16]), a_tail[:], COPY)
+
+        bank_a2 = ps.tile([P, 512], F32, name="bank_a2")
+        product_a(bank_a2[:, 0:J], 1)
+        a_1 = tile([P, J], F32, "a_1")
+        nc.vector.tensor_copy(a_1[:], bank_a2[:, 0:J])
+        nc.scalar.activation(pages[1][:].indirect(list_page[:]), a_1[:], COPY)
+
+        w2s_dealt = tile([P, R], U8, "w2s_dealt", "ws_first")
+        nc.vector.tensor_copy(w2s_dealt[:].rearrange("p (t m) -> p t m", t=PACK), w2s_raw[:].rearrange("p (m t) -> p t m", t=PACK))
+
+        bank_a3 = ps.tile([P, 512], F32, name="bank_a3")
+        product_a(bank_a3[:, 0:J], 2)
+        product_a(bank_a3[:, J : 2 * J], 3)
+        a_23 = tile([P, 2 * J], F32, "a_23")
+        nc.vector.tensor_copy(a_23[:], bank_a3[:])
+        for t in (2, 3):
+            nc.scalar.activation(pages[t][:].indirect(list_page[:]), a_23[:, (t - 2) * J : (t - 1) * J], COPY)
+
+        b_rows = [tile([P, J], F32, "b%d" % t) for t in range(PACK)]
+        for pair in range(2):
+            bank_b = ps.tile([P, 512], F32, name="bank_b%d" % pair)
+            for u in range(2):
+                cols = slice((2 * pair + u) * P, (2 * pair + u + 1) * P)
+                product(bank_b[:, u * J : (u + 1) * J], w2_dealt[:, cols].bitcast(FP8X4), w2s_dealt[:, cols], x_words[:], x_scales[:])
+            for u in range(2):
+                nc.vector.tensor_copy(b_rows[2 * pair + u][:], bank_b[:, u * J : (u + 1) * J])
+
+        v_words = tile([P, N], U32, "v_words", "w2_dealt")
+        v_scales = tile([P, N], U8, "v_scales", "ws_first")
+        nc.vector.tensor_copy(v_scales[:], vs_all[:].indirect(list_v[:]))
+        nc.vector.tensor_copy(v_words[:], v_all[:].indirect(list_v[:]))
+
+        picks = tile([P, PACK, O], F32, "picks")
+        for t in range(PACK):
+            nc.scalar.activation(picks[:, t, :], b_rows[t][:].indirect(list_pick[:]), COPY, scale=sa_t[:, t : t + 1])
+
+        parts = [slice(0, PAGE_PART), slice(PAGE_PART, C), slice(C, D)]
+        early = PACK - 1
+        rounded = tile([P, early, C], BF16, "rounded")
+        hid = [tile([P, part.stop - part.start, PACK], BF16, "hid%d" % i, tag) for i, (part, tag) in enumerate(zip(parts, ("v_all", "vs_all", "v_all")))]
+        for t in range(early):
+            nc.gpsimd.tensor_scalar(rounded[:, t, :], pages[t][:], 1.0, 0.0, MULT, ADD)
+        for i in range(2):
+            nc.vector.tensor_copy(
+                hid[i][:, :, 0:early].rearrange("p (c i) t -> p c t i", i=4),
+                rounded[:, :, parts[i]].rearrange("p t (c i) -> p c t i", i=4),
+            )
+        for i in range(2):
+            nc.vector.tensor_copy(hid[i][:, :, early], pages[early][:, parts[i]])
+
+        out_rows = out.rearrange("(h p) d -> p h d", p=P)
+
+        def finish(i, bank_name, evacuate):
+            width = parts[i].stop - parts[i].start
+            h_words = tile([P, width], U32, "h_words%d" % i)
+            h_scales = tile([P, width], U8, "h_scales%d" % i)
+            nc.vector.quantize_mx(out=h_words[:].bitcast(FP8X4), scales=h_scales[:], in_=hid[i][:].rearrange("p c t -> p (c t)"))
+            bank = ps.tile([P, 512], F32, name=bank_name)
+            for h in range(N // P):
+                cols = slice(h * P, (h + 1) * P)
+                product(bank[:, h * width : (h + 1) * width], v_words[:, cols].bitcast(FP8X4), v_scales[:, cols], h_words[:], h_scales[:])
+            y = tile([P, N // P, width], F32, "y%d" % i)
+            evacuate(y[:].rearrange("p h c -> p (h c)"), bank[:, 0 : 2 * width])
+            nc.sync.dma_start(out=out_rows[:, :, parts[i]], in_=y[:])
+
+        finish(0, "bank_y0", nc.scalar.copy)
+        finish(1, "bank_y1", nc.scalar.copy)
+        nc.vector.tensor_copy(hid[2][:], picks[:].rearrange("p t o -> p o t"))
+        finish(2, "bank_a0", nc.vector.tensor_copy)

@@ -20,7 +20,7 @@ ADD = mybir.AluOpType.add
 P = 128
 PACK = 4
 HALF = J // 2
-PAGE_PART = C // 2
+PAGE_HALF = C // 2
 
 
 def tile_picked_tokens_plain_twin_pageandpicks_store_plain_kernel(
@@ -31,6 +31,8 @@ def tile_picked_tokens_plain_twin_pageandpicks_store_plain_kernel(
     with ExitStack() as ctx:
         sb = ctx.enter_context(tc.tile_pool(name="sb", bufs=1))
         ps = ctx.enter_context(tc.psum_pool(name="ps", bufs=1))
+
+        shared = ctx.enter_context(tc.tile_pool(name="shared", bufs=1))
 
         def tile(shape, dtype, name, tag=None):
             return sb.tile(shape, dtype, name=name, tag=tag or name, align_bytes=64)
@@ -53,7 +55,7 @@ def tile_picked_tokens_plain_twin_pageandpicks_store_plain_kernel(
         list_pick = tile([P, O // 16], U16, "list_pick")
         list_v = tile([P, N // 16], U16, "list_v")
 
-        xs_stage = tile([64, 2 * T // 4], I32, "xs_stage")
+        xs_stage = tile([4, 4, T // 4], I32, "xs_stage")
         ws_stage = tile([P, 2 * R], U8, "ws_stage")
         xs_all = tile([P, T], U8, "xs_all")
         x_all = tile([P, T], U32, "x_all")
@@ -63,34 +65,37 @@ def tile_picked_tokens_plain_twin_pageandpicks_store_plain_kernel(
         v_all = tile([P, S], U32, "v_all")
         vs_all = tile([P, S], U8, "vs_all")
         sa_t = tile([P, PACK], F32, "sa_t")
-        pages = [tile([P, C], F32, "page%d" % t) for t in range(PACK)]
+        pages = [
+            shared.tile([P, C], F32, name="page%d" % t, align_bytes=64, offset=(t - 1) * 4 * C) if t in (1, 2) else tile([P, C], F32, "page%d" % t)
+            for t in range(PACK)
+        ]
 
         ws_words = ws_stage[:].bitcast(I32)
-        nc.vector.memset(xs_stage[:], 0)
-        nc.gpsimd.memset(ws_words[0:64], 0)
+        nc.vector.memset(ws_words[0:64], 0)
+        nc.gpsimd.memset(vs_all[:].bitcast(I32), 0)
+        load_scale_rows(nc.gpsimd, vs_all, vs_scales)
 
         nc.sync.dma_start(list_x[:], offs)
-        load_scale_pairs(nc.sync, xs_stage[:], xt_scales)
-        load_scale_pairs(nc.sync, ws_words, w_scales)
+        nc.sync.dma_start(out=xs_stage[:], in_=xt_scales[0].bitcast(I32).rearrange("(q i) c -> i q c", i=4))
         nc.sync.dma_start(out=x_all[:].bitcast(I32), in_=words_of(xt_words))
-        nc.sync.dma_start(out=w_raw[:].bitcast(I32), in_=w_words[0].bitcast(I32))
-        nc.sync.dma_start(out=w2_raw[:].bitcast(I32), in_=words_of(w2_words))
+        nc.scalar.dma_start(out=w_raw[:].bitcast(I32), in_=w_words[0].bitcast(I32))
+        load_scale_pairs(nc.scalar, ws_words, w_scales)
         nc.sync.dma_start(list_page[:], offs2)
+        nc.sync.dma_start(out=w2_raw[:].bitcast(I32), in_=words_of(w2_words))
 
+        nc.vector.memset(xs_all[:].bitcast(I32), 0)
         nc.vector.memset(w2s_raw[:].bitcast(I32), 0)
-        nc.vector.memset(vs_all[:].bitcast(I32), 0)
         for page in pages:
             nc.vector.memset(page[:], 0.0)
 
         load_scale_rows(nc.sync, w2s_raw, w2_scales)
         nc.sync.dma_start(list_v[:], offs4)
         nc.sync.dma_start(out=v_all[:].bitcast(I32), in_=words_of(vs_words))
-        load_scale_rows(nc.gpsimd, vs_all, vs_scales)
         nc.sync.dma_start(list_pick[:], offs3)
-        nc.gpsimd.dma_start(out=sa_t[:], in_=sa.rearrange("(p t) o -> p (t o)", t=PACK))
+        nc.sync.dma_start(out=sa_t[:], in_=sa.rearrange("(p t) o -> p (t o)", t=PACK))
 
-        for h in range(2):
-            nc.vector.tensor_copy(xs_all[64 * h : 64 * h + 64, :].bitcast(I32), xs_stage[:, h * T // 4 : (h + 1) * T // 4])
+        for q in range(4):
+            nc.vector.tensor_copy(xs_all[32 * q : 32 * q + 4, :].bitcast(I32), xs_stage[:, q, :])
         nc.vector.tensor_copy(ws_words[64:128, 0 : R // 4], ws_words[0:64, R // 4 : 2 * R // 4])
 
         x_words = tile([P, J], U32, "x_words")
@@ -99,7 +104,6 @@ def tile_picked_tokens_plain_twin_pageandpicks_store_plain_kernel(
         ws_first = tile([P, P], U8, "ws_first")
         w_rest = tile([P, 2 * (R - P)], U8, "w_rest")
         ws_rest = tile([P, R - P], U8, "ws_rest")
-        w2_dealt = tile([P, R], U32, "w2_dealt")
 
         w_by_t = w_raw[:].bitcast(U16).rearrange("p (m t) -> p t m", t=PACK)
         ws_by_t = ws_stage[:, 0:R].rearrange("p (m t) -> p t m", t=PACK)
@@ -119,9 +123,8 @@ def tile_picked_tokens_plain_twin_pageandpicks_store_plain_kernel(
         gather_x(first)
         bank_a0 = ps.tile([P, 512], F32, name="bank_a0")
         product(bank_a0[:, 0:HALF], w_first[:].bitcast(FP4X4), ws_first[:], x_words[:, first], x_scales[:, first])
-        a_head = tile([P, HALF], F32, "a_head", "w2_raw")
+        a_head = tile([P, HALF], F32, "a_head")
         nc.scalar.copy(w_rest[:].bitcast(U16).rearrange("p (t m) -> p t m", m=P), w_by_t[:, 1:PACK, :])
-        nc.scalar.copy(w2_dealt[:].rearrange("p (t m) -> p t m", t=PACK), w2_raw[:].rearrange("p (m t) -> p t m", t=PACK))
         nc.scalar.copy(a_head[:], bank_a0[:, 0:HALF])
         nc.scalar.activation(pages[0][:].indirect(list_page[:, 0 : HALF // 16]), a_head[:], COPY)
 
@@ -144,9 +147,6 @@ def tile_picked_tokens_plain_twin_pageandpicks_store_plain_kernel(
         nc.vector.tensor_copy(a_1[:], bank_a2[:, 0:J])
         nc.scalar.activation(pages[1][:].indirect(list_page[:]), a_1[:], COPY)
 
-        w2s_dealt = tile([P, R], U8, "w2s_dealt", "ws_first")
-        nc.vector.tensor_copy(w2s_dealt[:].rearrange("p (t m) -> p t m", t=PACK), w2s_raw[:].rearrange("p (m t) -> p t m", t=PACK))
-
         bank_a3 = ps.tile([P, 512], F32, name="bank_a3")
         product_a(bank_a3[:, 0:J], 2)
         product_a(bank_a3[:, J : 2 * J], 3)
@@ -155,54 +155,72 @@ def tile_picked_tokens_plain_twin_pageandpicks_store_plain_kernel(
         for t in (2, 3):
             nc.scalar.activation(pages[t][:].indirect(list_page[:]), a_23[:, (t - 2) * J : (t - 1) * J], COPY)
 
-        b_rows = [tile([P, J], F32, "b%d" % t) for t in range(PACK)]
-        for pair in range(2):
-            bank_b = ps.tile([P, 512], F32, name="bank_b%d" % pair)
-            for u in range(2):
-                cols = slice((2 * pair + u) * P, (2 * pair + u + 1) * P)
-                product(bank_b[:, u * J : (u + 1) * J], w2_dealt[:, cols].bitcast(FP8X4), w2s_dealt[:, cols], x_words[:], x_scales[:])
-            for u in range(2):
-                nc.vector.tensor_copy(b_rows[2 * pair + u][:], bank_b[:, u * J : (u + 1) * J])
+        w2_dealt = tile([P, R], U32, "w2_dealt", "w_rest")
+        nc.vector.tensor_copy(w2_dealt[:].rearrange("p (t m) -> p t m", t=PACK), w2_raw[:].rearrange("p (m t) -> p t m", t=PACK))
 
-        v_words = tile([P, N], U32, "v_words", "w2_dealt")
-        v_scales = tile([P, N], U8, "v_scales", "ws_first")
-        nc.vector.tensor_copy(v_scales[:], vs_all[:].indirect(list_v[:]))
+        w2s_dealt = tile([P, R], U8, "w2s_dealt", "ws_rest")
+        nc.vector.tensor_copy(w2s_dealt[:].rearrange("p (t m) -> p t m", t=PACK), w2s_raw[:].rearrange("p (m t) -> p t m", t=PACK))
+
+        v_words = tile([P, N], U32, "v_words", "w2_raw")
+        v_scales = tile([P, N], U8, "v_scales", "w2s_raw")
         nc.vector.tensor_copy(v_words[:], v_all[:].indirect(list_v[:]))
+        nc.vector.tensor_copy(v_scales[:], vs_all[:].indirect(list_v[:]))
+
+        b_rows = [tile([P, J], F32, "b%d" % t) for t in range(PACK)]
+        banks_b = [ps.tile([P, 512], F32, name="bank_b%d" % pair) for pair in range(2)]
+        b_sums = [banks_b[t // 2][:, t % 2 * J : (t % 2 + 1) * J] for t in range(PACK)]
+        for t in range(PACK):
+            cols = slice(t * P, (t + 1) * P)
+            product(b_sums[t], w2_dealt[:, cols].bitcast(FP8X4), w2s_dealt[:, cols], x_words[:], x_scales[:])
+
+        for t in range(PACK):
+            nc.vector.tensor_copy(b_rows[t][:], b_sums[t])
 
         picks = tile([P, PACK, O], F32, "picks")
         for t in range(PACK):
             nc.scalar.activation(picks[:, t, :], b_rows[t][:].indirect(list_pick[:]), COPY, scale=sa_t[:, t : t + 1])
 
-        parts = [slice(0, PAGE_PART), slice(PAGE_PART, C), slice(C, D)]
         early = PACK - 1
-        rounded = tile([P, early, C], BF16, "rounded")
-        hid = [tile([P, part.stop - part.start, PACK], BF16, "hid%d" % i, tag) for i, (part, tag) in enumerate(zip(parts, ("v_all", "vs_all", "v_all")))]
-        for t in range(early):
+        halves = [slice(0, PAGE_HALF), slice(PAGE_HALF, C)]
+        rounded = tile([P, early, C], BF16, "rounded", "x_words")
+        for t in range(early - 1):
             nc.gpsimd.tensor_scalar(rounded[:, t, :], pages[t][:], 1.0, 0.0, MULT, ADD)
-        for i in range(2):
-            nc.vector.tensor_copy(
-                hid[i][:, :, 0:early].rearrange("p (c i) t -> p c t i", i=4),
-                rounded[:, :, parts[i]].rearrange("p t (c i) -> p c t i", i=4),
-            )
-        for i in range(2):
-            nc.vector.tensor_copy(hid[i][:, :, early], pages[early][:, parts[i]])
+        nc.vector.tensor_copy(rounded[:, early - 1, :], pages[early - 1][:])
+        hid = shared.tile([P, C, PACK], BF16, name="hid", align_bytes=64, offset=0)
+        nc.vector.tensor_copy(hid[:, :, 0:early], rounded[:].rearrange("p t c -> p c t"))
+        for half in halves:
+            nc.vector.tensor_copy(hid[:, half, early], pages[early][:, half])
 
-        out_rows = out.rearrange("(h p) d -> p h d", p=P)
+        def quantise(values, name, tag=None):
+            width = values.shape[1]
+            h_words = tile([P, width], U32, name + "_words", tag)
+            h_scales = tile([P, width], U8, name + "_scales")
+            nc.vector.quantize_mx(out=h_words[:].bitcast(FP8X4), scales=h_scales[:], in_=values.rearrange("p c t -> p (c t)"))
+            return h_words, h_scales
 
-        def finish(i, bank_name, evacuate):
-            width = parts[i].stop - parts[i].start
-            h_words = tile([P, width], U32, "h_words%d" % i)
-            h_scales = tile([P, width], U8, "h_scales%d" % i)
-            nc.vector.quantize_mx(out=h_words[:].bitcast(FP8X4), scales=h_scales[:], in_=hid[i][:].rearrange("p c t -> p (c t)"))
+        def product_y(acc, h, operand):
+            cols = slice(h * P, (h + 1) * P)
+            product(acc, v_words[:, cols].bitcast(FP8X4), v_scales[:, cols], operand[0][:], operand[1][:])
+
+        def finish_page(i, h, operand, bank_name, evacuate):
             bank = ps.tile([P, 512], F32, name=bank_name)
-            for h in range(N // P):
-                cols = slice(h * P, (h + 1) * P)
-                product(bank[:, h * width : (h + 1) * width], v_words[:, cols].bitcast(FP8X4), v_scales[:, cols], h_words[:], h_scales[:])
-            y = tile([P, N // P, width], F32, "y%d" % i)
-            evacuate(y[:].rearrange("p h c -> p (h c)"), bank[:, 0 : 2 * width])
-            nc.sync.dma_start(out=out_rows[:, :, parts[i]], in_=y[:])
+            product_y(bank[:, 0:PAGE_HALF], h, operand)
+            y = tile([P, PAGE_HALF], F32, "y%d%d" % (i, h))
+            evacuate(y[:], bank[:, 0:PAGE_HALF])
+            nc.sync.dma_start(out=out[h * P : (h + 1) * P, halves[i]], in_=y[:])
 
-        finish(0, "bank_y0", nc.scalar.copy)
-        finish(1, "bank_y1", nc.scalar.copy)
-        nc.vector.tensor_copy(hid[2][:], picks[:].rearrange("p t o -> p o t"))
-        finish(2, "bank_a0", nc.vector.tensor_copy)
+        hid_picks = tile([P, O, PACK], BF16, "hid_picks")
+        nc.scalar.copy(hid_picks[:], picks[:].rearrange("p t o -> p o t"))
+        page_low = quantise(hid[:, halves[0], :], "low")
+        finish_page(0, 0, page_low, "bank_y0", nc.scalar.copy)
+        finish_page(0, 1, page_low, "bank_y1", nc.scalar.copy)
+        page_high = quantise(hid[:, halves[1], :], "high")
+        picked = quantise(hid_picks[:], "picked", "page%d" % early)
+        finish_page(1, 0, page_high, "bank_a0", nc.vector.tensor_copy)
+        finish_page(1, 1, page_high, "bank_a1", nc.vector.tensor_copy)
+        bank = ps.tile([P, 512], F32, name="bank_a2")
+        for h in range(N // P):
+            product_y(bank[:, h * O : (h + 1) * O], h, picked)
+        y = tile([P, N // P, O], F32, "y_picks")
+        nc.scalar.copy(y[:].rearrange("p h c -> p (h c)"), bank[:, 0 : N // P * O])
+        nc.scalar.dma_start(out=out.rearrange("(h p) d -> p h d", p=P)[:, :, C:D], in_=y[:])

from contextlib import ExitStack

import concourse.mybir as mybir

K, J, R, T, C, O, D, N, S = 512, 256, 512, 512, 512, 128, 640, 256, 1024
FLOPS = 2 * (2 * K * R * J + R * N * D)

F32 = mybir.dt.float32
BF16 = mybir.dt.bfloat16
I32 = mybir.dt.int32
U32 = mybir.dt.uint32
U16 = mybir.dt.uint16
U8 = mybir.dt.uint8
FP8X4 = mybir.dt.float8_e4m3fn_x4
FP4X4 = mybir.dt.float4_e2m1fn_x4
COPY = mybir.ActivationFunctionType.Copy
MULT = mybir.AluOpType.mult
ADD = mybir.AluOpType.add

P = 128
PACK = 4
HALF = J // 2
PAGE_HALF = C // 2


def tile_picked_tokens_plain_twin_pageandpicks_store_plain_kernel(
    tc, xt_words, xt_scales, w_words, w_scales, w2_words, w2_scales, sa, vs_words, vs_scales, offs, offs2, offs3, offs4, out
):
    nc = tc.nc

    with ExitStack() as ctx:
        sb = ctx.enter_context(tc.tile_pool(name="sb", bufs=1))
        ps = ctx.enter_context(tc.psum_pool(name="ps", bufs=1))

        shared = ctx.enter_context(tc.tile_pool(name="shared", bufs=1))

        def tile(shape, dtype, name, tag=None):
            return sb.tile(shape, dtype, name=name, tag=tag or name, align_bytes=64)

        def words_of(dram):
            return dram[0].rearrange("p n t -> p (n t)").bitcast(I32)

        def load_scale_pairs(queue, stage, dram):
            rows = dram[0].bitcast(I32).rearrange("(h g i) c -> g i h c", h=2, g=2)
            for g in range(2):
                queue.dma_start(out=stage[32 * g : 32 * g + 4].rearrange("i (h c) -> i h c", h=2), in_=rows[g])

        def load_scale_rows(queue, plane, dram):
            rows = dram[0].bitcast(I32)
            for q in range(4):
                queue.dma_start(out=plane[32 * q : 32 * q + 4, :].bitcast(I32), in_=rows[4 * q : 4 * q + 4, :])

        list_x = tile([P, J // 16], U16, "list_x")
        list_page = tile([P, J // 16], U16, "list_page")
        list_pick = tile([P, O // 16], U16, "list_pick")
        list_v = tile([P, N // 16], U16, "list_v")

        xs_stage = tile([4, 4, T // 4], I32, "xs_stage")
        ws_stage = tile([P, 2 * R], U8, "ws_stage")
        xs_all = tile([P, T], U8, "xs_all")
        x_all = tile([P, T], U32, "x_all")
        w_raw = tile([P, 2 * R], U8, "w_raw")
        w2_raw = tile([P, R], U32, "w2_raw")
        w2s_raw = tile([P, R], U8, "w2s_raw")
        v_all = tile([P, S], U32, "v_all")
        vs_all = tile([P, S], U8, "vs_all")
        sa_t = tile([P, PACK], F32, "sa_t")
        pages = [
            shared.tile([P, C], F32, name="page%d" % t, align_bytes=64, offset=(t - 1) * 4 * C) if t in (1, 2) else tile([P, C], F32, "page%d" % t)
            for t in range(PACK)
        ]

        ws_words = ws_stage[:].bitcast(I32)
        nc.vector.memset(ws_words[0:64], 0)
        nc.gpsimd.memset(vs_all[:].bitcast(I32), 0)
        load_scale_rows(nc.gpsimd, vs_all, vs_scales)

        nc.sync.dma_start(list_x[:], offs)
        nc.sync.dma_start(out=xs_stage[:], in_=xt_scales[0].bitcast(I32).rearrange("(q i) c -> i q c", i=4))
        nc.sync.dma_start(out=x_all[:].bitcast(I32), in_=words_of(xt_words))
        nc.scalar.dma_start(out=w_raw[:].bitcast(I32), in_=w_words[0].bitcast(I32))
        load_scale_pairs(nc.scalar, ws_words, w_scales)
        nc.sync.dma_start(list_page[:], offs2)
        nc.sync.dma_start(out=w2_raw[:].bitcast(I32), in_=words_of(w2_words))

        nc.vector.memset(xs_all[:].bitcast(I32), 0)
        nc.vector.memset(w2s_raw[:].bitcast(I32), 0)
        for page in pages:
            nc.vector.memset(page[:], 0.0)

        load_scale_rows(nc.sync, w2s_raw, w2_scales)
        nc.sync.dma_start(list_v[:], offs4)
        nc.sync.dma_start(out=v_all[:].bitcast(I32), in_=words_of(vs_words))
        nc.sync.dma_start(list_pick[:], offs3)
        nc.sync.dma_start(out=sa_t[:], in_=sa.rearrange("(p t) o -> p (t o)", t=PACK))

        for q in range(4):
            nc.vector.tensor_copy(xs_all[32 * q : 32 * q + 4, :].bitcast(I32), xs_stage[:, q, :])
        nc.vector.tensor_copy(ws_words[64:128, 0 : R // 4], ws_words[0:64, R // 4 : 2 * R // 4])

        x_words = tile([P, J], U32, "x_words")
        x_scales = tile([P, J], U8, "x_scales")
        w_first = tile([P, 2 * P], U8, "w_first")
        ws_first = tile([P, P], U8, "ws_first")
        w_rest = tile([P, 2 * (R - P)], U8, "w_rest")
        ws_rest = tile([P, R - P], U8, "ws_rest")

        w_by_t = w_raw[:].bitcast(U16).rearrange("p (m t) -> p t m", t=PACK)
        ws_by_t = ws_stage[:, 0:R].rearrange("p (m t) -> p t m", t=PACK)

        def gather_x(cols):
            entries = list_x[:, cols.start // 16 : cols.stop // 16]
            nc.vector.tensor_copy(x_scales[:, cols], xs_all[:].indirect(entries))
            nc.vector.tensor_copy(x_words[:, cols], x_all[:].indirect(entries))

        def product(acc, lhs_words, lhs_scales, rhs_words, rhs_scales):
            nc.tensor.matmul_mx(out=acc, lhsT=lhs_words, lhsT_scale=lhs_scales, rhs=rhs_words.bitcast(FP8X4), rhs_scale=rhs_scales, start=True, stop=True)

        first, second = slice(0, HALF), slice(HALF, J)

        nc.scalar.copy(w_first[:].bitcast(U16), w_by_t[:, 0, :])
        nc.vector.tensor_copy(ws_first[:], ws_by_t[:, 0, :])
        gather_x(first)
        bank_a0 = ps.tile([P, 512], F32, name="bank_a0")
        product(bank_a0[:, 0:HALF], w_first[:].bitcast(FP4X4), ws_first[:], x_words[:, first], x_scales[:, first])
        a_head = tile([P, HALF], F32, "a_head")
        nc.scalar.copy(w_rest[:].bitcast(U16).rearrange("p (t m) -> p t m", m=P), w_by_t[:, 1:PACK, :])
        nc.scalar.copy(a_head[:], bank_a0[:, 0:HALF])
        nc.scalar.activation(pages[0][:].indirect(list_page[:, 0 : HALF // 16]), a_head[:], COPY)

        gather_x(second)
        nc.vector.tensor_copy(ws_rest[:].rearrange("p (t m) -> p t m", m=P), ws_by_t[:, 1:PACK, :])

        def product_a(acc, t):
            cols = slice((t - 1) * P, t * P)
            product(acc, w_rest[:, 2 * cols.start : 2 * cols.stop].bitcast(FP4X4), ws_rest[:, cols], x_words[:], x_scales[:])

        bank_a1 = ps.tile([P, 512], F32, name="bank_a1")
        product(bank_a1[:, 0:HALF], w_first[:].bitcast(FP4X4), ws_first[:], x_words[:, second], x_scales[:, second])
        a_tail = tile([P, HALF], F32, "a_tail")
        nc.vector.tensor_copy(a_tail[:], bank_a1[:, 0:HALF])
        nc.scalar.activation(pages[0][:].indirect(list_page[:, HALF // 16 : J // 16]), a_tail[:], COPY)

        bank_a2 = ps.tile([P, 512], F32, name="bank_a2")
        product_a(bank_a2[:, 0:J], 1)
        a_1 = tile([P, J], F32, "a_1")
        nc.vector.tensor_copy(a_1[:], bank_a2[:, 0:J])
        nc.scalar.activation(pages[1][:].indirect(list_page[:]), a_1[:], COPY)

        bank_a3 = ps.tile([P, 512], F32, name="bank_a3")
        product_a(bank_a3[:, 0:J], 2)
        product_a(bank_a3[:, J : 2 * J], 3)
        a_23 = tile([P, 2 * J], F32, "a_23")
        nc.vector.tensor_copy(a_23[:], bank_a3[:])
        for t in (2, 3):
            nc.scalar.activation(pages[t][:].indirect(list_page[:]), a_23[:, (t - 2) * J : (t - 1) * J], COPY)

        w2_dealt = tile([P, R], U32, "w2_dealt", "w_rest")
        nc.vector.tensor_copy(w2_dealt[:].rearrange("p (t m) -> p t m", t=PACK), w2_raw[:].rearrange("p (m t) -> p t m", t=PACK))

        w2s_dealt = tile([P, R], U8, "w2s_dealt", "ws_rest")
        nc.vector.tensor_copy(w2s_dealt[:].rearrange("p (t m) -> p t m", t=PACK), w2s_raw[:].rearrange("p (m t) -> p t m", t=PACK))

        v_words = tile([P, N], U32, "v_words", "w2_raw")
        v_scales = tile([P, N], U8, "v_scales", "w2s_raw")
        nc.vector.tensor_copy(v_words[:], v_all[:].indirect(list_v[:]))
        nc.vector.tensor_copy(v_scales[:], vs_all[:].indirect(list_v[:]))

        b_rows = [tile([P, J], F32, "b%d" % t) for t in range(PACK)]
        banks_b = [ps.tile([P, 512], F32, name="bank_b%d" % pair) for pair in range(2)]
        b_sums = [banks_b[t // 2][:, t % 2 * J : (t % 2 + 1) * J] for t in range(PACK)]
        for t in range(PACK):
            cols = slice(t * P, (t + 1) * P)
            product(b_sums[t], w2_dealt[:, cols].bitcast(FP8X4), w2s_dealt[:, cols], x_words[:], x_scales[:])

        for t in range(PACK):
            nc.vector.tensor_copy(b_rows[t][:], b_sums[t])

        picks = tile([P, PACK, O], F32, "picks")
        for t in range(PACK):
            nc.scalar.activation(picks[:, t, :], b_rows[t][:].indirect(list_pick[:]), COPY, scale=sa_t[:, t : t + 1])

        early = PACK - 1
        halves = [slice(0, PAGE_HALF), slice(PAGE_HALF, C)]
        rounded = tile([P, early, C], BF16, "rounded", "x_words")
        for t in range(early - 1):
            nc.gpsimd.tensor_scalar(rounded[:, t, :], pages[t][:], 1.0, 0.0, MULT, ADD)
        nc.vector.tensor_copy(rounded[:, early - 1, :], pages[early - 1][:])
        hid = shared.tile([P, C, PACK], BF16, name="hid", align_bytes=64, offset=0)
        nc.vector.tensor_copy(hid[:, :, 0:early], rounded[:].rearrange("p t c -> p c t"))
        for half in halves:
            nc.vector.tensor_copy(hid[:, half, early], pages[early][:, half])

        def quantise(values, name, tag=None):
            width = values.shape[1]
            h_words = tile([P, width], U32, name + "_words", tag)
            h_scales = tile([P, width], U8, name + "_scales")
            nc.vector.quantize_mx(out=h_words[:].bitcast(FP8X4), scales=h_scales[:], in_=values.rearrange("p c t -> p (c t)"))
            return h_words, h_scales

        def product_y(acc, h, operand):
            cols = slice(h * P, (h + 1) * P)
            product(acc, v_words[:, cols].bitcast(FP8X4), v_scales[:, cols], operand[0][:], operand[1][:])

        def finish_page(i, h, operand, bank_name, evacuate):
            bank = ps.tile([P, 512], F32, name=bank_name)
            product_y(bank[:, 0:PAGE_HALF], h, operand)
            y = tile([P, PAGE_HALF], F32, "y%d%d" % (i, h))
            evacuate(y[:], bank[:, 0:PAGE_HALF])
            nc.sync.dma_start(out=out[h * P : (h + 1) * P, halves[i]], in_=y[:])

        hid_picks = tile([P, O, PACK], BF16, "hid_picks")
        nc.scalar.copy(hid_picks[:], picks[:].rearrange("p t o -> p o t"))
        page_low = quantise(hid[:, halves[0], :], "low")
        finish_page(0, 0, page_low, "bank_y0", nc.scalar.copy)
        finish_page(0, 1, page_low, "bank_y1", nc.scalar.copy)
        page_high = quantise(hid[:, halves[1], :], "high")
        picked = quantise(hid_picks[:], "picked", "page%d" % early)
        finish_page(1, 0, page_high, "bank_a0", nc.vector.tensor_copy)
        finish_page(1, 1, page_high, "bank_a1", nc.vector.tensor_copy)
        bank = ps.tile([P, 512], F32, name="bank_a2")
        for h in range(N // P):
            product_y(bank[:, h * O : (h + 1) * O], h, picked)
        y = tile([P, N // P, O], F32, "y_picks")
        nc.scalar.copy(y[:].rearrange("p h c -> p (h c)"), bank[:, 0 : N // P * O])
        nc.scalar.dma_start(out=out.rearrange("(h p) d -> p h d", p=P)[:, :, C:D], in_=y[:])
